import numpy as np
CORES = [24,48,72,152,176,200]
N = 6
T, KB = 1024, 64
def entries(a): return a.T.reshape(-1)
def pack(v, P): return np.ascontiguousarray(np.asarray(v, np.int32).reshape(-1, P).T)
def order(K):
    return np.argsort(K, kind="stable")
def lists(rng, how):
    K = rng.integers(0, KB, (N, T)); i = np.arange(N)
    if how == "astride":
        s, m, k = rng.integers(1, N), rng.integers(T // 4, 3 * T // 4), np.sort(rng.permutation(KB)[:3])
        K = np.repeat(np.where(i >= s, k[1], k[2])[:, None], T, axis=1); K[s - 1, rng.permutation(T)[:m]] = k[0]
    if how == "skew": K = np.stack([rng.choice(KB, T, p=rng.dirichlet(np.ones(KB) * 0.5)) for r in range(N)])
    if how[:4] == "turn":
        s = rng.choice(i[1:][ord(how[-1]) - 97::3]); K = ((i + s) % N * KB // N)[:, None] + rng.integers(0, max(KB // N, 1), (N, T))
    return {"key": np.stack([pack(k, 16) for k in K])}
def setup_inputs(rng):
    return dict({"x": rng.standard_normal((N, 128, T), dtype=np.float32)}, **lists(rng, "uniform"))
def setup_inputs_astride(rng):
    d = setup_inputs(rng); d.update(lists(rng, "astride"))
    for k in ("x",): d[k] = (d[k].astype(np.float32) * 1048576.0).astype(d[k].dtype)
    return d
def setup_inputs_skew(rng):
    d = setup_inputs(rng); d.update(lists(rng, "skew"))
    for k in ("x",): d[k] = (d[k].astype(np.float32) * (1 / 1024.0)).astype(d[k].dtype)
    return d
def setup_inputs_turna(rng):
    d = setup_inputs(rng); d.update(lists(rng, "turna"))
    return d
def setup_inputs_turnb(rng):
    d = setup_inputs(rng); d.update(lists(rng, "turnb"))
    return d
def setup_inputs_turnc(rng):
    d = setup_inputs(rng); d.update(lists(rng, "turnc"))
    return d
def check_inputs(x):
    bad = []
    if x["key"].min() < 0 or x["key"].max() >= KB: bad.append("key out of range")
    return bad
def reference(x, key):
    X = np.concatenate(list(x), axis=1); K = np.concatenate([entries(a) for a in key])
    Y = X[:, order(K)]
    return {"y": np.stack([Y[:, T * r:T * r + T] for r in range(N)])}

@@ -1,0 +1,297 @@
+from concourse.bass import DstId, RemoteDMATransfer
+from concourse.mybir import AluOpType as OP, AxisListType, ActivationFunctionType as ACT
+
+NR, TC, NK = 6, 1024, 64
+F32, F16, I32, U16 = "float32", "float16", "int32", "uint16"
+
+SCRATCH = {
+    "XW": ("sbuf", [128, NR * TC], F32),
+    "yS": ("sbuf", [128, TC], F32),
+    "Lw": ("sbuf", [128, NR * 64], F32),
+    "Cc": ("sbuf", [128, NR * 4], F32),
+    "kS": ("sbuf", [16, 64], I32),
+    "II": ("sbuf", [128, 128], I32), "PI4": ("sbuf", [128, 4], I32), "PJ": ("sbuf", [128, 4], I32),
+    "JI": ("sbuf", [128, 8], F32), "PC": ("sbuf", [128, 4], F32), "IH": ("sbuf", [128, 128], F16),
+    "M16i": ("sbuf", [128, 128], I32), "M16": ("sbuf", [128, 128], F16), "mh": ("sbuf", [16, 2], F32),
+    "R8": ("sbuf", [16, 8], F16), "SL": ("sbuf", [128, 128], F16), "SU": ("sbuf", [128, 128], F16),
+    "on4": ("sbuf", [128, 4], F16), "kl": ("sbuf", [16, 128], F16), "O": ("sbuf", [128, 512], F16),
+    "S": ("sbuf", [128, 512], F16), "LE2": ("sbuf", [128, 128], F16), "LEs": ("sbuf", [128, 64], F16),
+    "SB": ("sbuf", [128, 512], F16), "Wk": ("sbuf", [128, 512], F16), "pos": ("sbuf", [128, 8], F32),
+    "pi": ("sbuf", [128, 8], I32), "hl": ("sbuf", [128, 16], I32), "hlF": ("sbuf", [128, 16], F32),
+    "Ah": ("sbuf", [128, 1024], F16), "Bh": ("sbuf", [128, 512], F16),
+    "id32": ("sbuf", [128, 128], F32), "shf": ("sbuf", [128, 128], F32), "e16": ("sbuf", [128, 128], F32),
+    "m8": ("sbuf", [128, 8], F32), "gI": ("sbuf", [128, 128], I32),
+    "Qc": ("sbuf", [128, 128], F32), "rst": ("sbuf", [128, 128], F32), "i1k": ("sbuf", [128, 1024], F16),
+    "on16": ("sbuf", [128, 16], F32), "rv": ("sbuf", [128, 96], F16),
+    "sm": ("sbuf", [128, 48], F32),
+    "U": ("sbuf", [128, 3 * 1024], F16), "f1": ("sbuf", [128, 128], F32), "fi": ("sbuf", [128, 128], I32),
+    "hi": ("sbuf", [128, 128], I32), "lo": ("sbuf", [128, 128], I32), "hm": ("sbuf", [128, 128], F32),
+    "lm": ("sbuf", [128, 128], F32), "off1": ("sbuf", [128, 8], U16), "G": ("sbuf", [128, 128], F32),
+    "GM": ("sbuf", [128, 128], F32), "GS": ("sbuf", [128, 128], F32), "lr": ("sbuf", [128, 64], F32),
+    "lst": ("sbuf", [128, 64], U16),
+}
+PX, SH, TG, TH, CS, DV, DR, PQ = 0, 8, 16, 20, 24, 32, 36, 40
+for _n in ("psA", "psB", "psH", "psL", "psV", "psO", "psG", "psF"):
+    SCRATCH[_n] = ("psum", [128, 512], F32)
+SEMAPHORES = ["kld", "x0", "x1", "x2", "x3", "harr", "larr", "xarr", "loc", "sv", "st", "sp", "sa", "ysy", "ysc"]
+
+
+def _engines(mask):
+    return bin(mask).count("1")
+
+
+def _plan(T, topo, src):
+    dests = [d for d in T.cores if d != src]
+    direct = [d for d in dests if topo.may_write(src, d)]
+    cross = [d for d in dests if not topo.may_write(src, d)]
+    first = src - src % 8
+    mine = [c for c in range(first, first + 8) if c != src and (topo.host(c), topo.chip(c)) == (topo.host(src), topo.chip(src))]
+    able = [c for c in mine if all(topo.may_write(c, d) for d in dests)]
+    near = [c for c in able if topo.die(c) == topo.die(src)]
+    far = [c for c in able if topo.die(c) != topo.die(src)]
+    relays = [c for pair in zip(near, far) for c in pair]
+    ni = (len(cross) + 1) // 2
+    widths = [192, 280, 280, 272] if ni == 1 else [192, 192, 320, 320]
+    starts = [sum(widths[:i]) for i in range(len(widths))]
+    idx = {relays[i]: cross[i::ni] for i in range(ni)}
+    return relays, starts, widths, idx, direct
+
+
+def rank_program(g, core, T, topo):
+    rank = T.rank_of(core)
+
+    def send(dests, mask, name, a, w, rsem):
+        ids = []
+        for d in dests:
+            rid, pnc = topo.addr(d, core)
+            ids.append(DstId(rid=rid, pnc=pnc))
+        ap = T[name][:, a:a + w]
+        g.remote_dma_fused([RemoteDMATransfer(dst_ids=ids, dma_engine_mask=mask, remote_sem=T.sem[rsem],
+                                              srcs=[ap], dsts=[ap for d in dests])], local_sem=T.sem.loc)
+        return _engines(mask)
+
+    if rank is None:
+        for r, src in enumerate(T.cores):
+            if (topo.host(src), topo.chip(src)) != (topo.host(core), topo.chip(core)):
+                continue
+            relays, starts, widths, idx, direct = _plan(T, topo, src)
+            if core not in relays:
+                return
+            i = relays.index(core)
+            dests = [d for d in T.cores if d != src]
+            dests = dests[i % 5:] + dests[:i % 5]
+            off = topo.mask(core, dests[0])
+            n = 0
+            if core in idx:
+                g.wait_ge(T.sem.harr, _engines(off))
+                n += send(idx[core], off, "Cc", 4 * r, 4, "harr")
+            g.wait_ge(T.sem.xarr, _engines(topo.mask(src, core) & ~topo.mask(src, direct[0])))
+            n += send(dests, off, "XW", TC * r + starts[i], widths[i], "xarr")
+            if core in idx:
+                g.wait_ge(T.sem.larr, _engines(off))
+                n += send(idx[core], off, "Lw", 64 * r, 64, "larr")
+            g.wait_ge(T.sem.loc, n)
+        return
+
+    relays, starts, widths, idx, direct = _plan(T, topo, core)
+    off = topo.mask(core, direct[0])
+    inner = topo.mask(core, relays[0]) & ~off
+    eng = {"v": g.vector, "t": g.tensor, "p": g, "a": g.scalar, "y": g.sync}
+    semof = {"v": "sv", "t": "st", "p": "sp", "a": "sa"}
+    cnt, seen, wr, rd = {}, {}, {}, {}
+
+    def need(q, toks):
+        best = {}
+        for s, n in toks:
+            best[s] = max(best.get(s, 0), n)
+        for s, n in best.items():
+            if seen.get((q, s), 0) < n:
+                eng[q].wait_ge(T.sem[s], n)
+                seen[(q, s)] = n
+
+    def reads(q, names):
+        need(q, [t for n in names for t in wr.get(n, [])])
+
+    def op(q, fn, rds, wrs, *args, inc=True, **kw):
+        toks = [t for n in rds for t in wr.get(n, [])]
+        for n in wrs:
+            toks += wr.get(n, []) + rd.get(n, [])
+        need(q, toks)
+        ins = fn(*args, **kw)
+        if inc:
+            s = semof[q]
+            ins.then_inc(T.sem[s], 1)
+            cnt[s] = cnt.get(s, 0) + 1
+            for n in rds:
+                rd.setdefault(n, []).append((s, cnt[s]))
+            for n in wrs:
+                wr[n] = [(s, cnt[s])]
+                rd[n] = []
+
+    v, t_, sm = g.vector, g.tensor, T.sm
+
+    def vts(o, i, s1, s2, o0, o1=None, R=(), W=()):
+        if o1 is None:
+            op("v", v.tensor_scalar, R, W, o, i, s1, s2, o0)
+        else:
+            op("v", v.tensor_scalar, R, W, o, i, s1, s2, o0, o1)
+
+    def vtt(o, a, b, o0, R=(), W=()):
+        op("v", v.tensor_tensor, R, W, o, a, b, o0)
+
+    def vcp(o, i, R=(), W=()):
+        op("v", v.tensor_copy, R, W, o, i)
+
+    def mm(o, l, r, R, W, start=True, stop=True):
+        op("t", t_.matmul, R, W if stop else (), o, l, r, start, stop, inc=stop)
+
+    g.sync.dma_start(T.kS[:], T.key[:]).then_inc(T.sem.kld, 16)
+    wr["kS"] = [("kld", 16)]
+    for i in range(4):
+        a, w = starts[i], widths[i]
+        (g.scalar if i % 2 == 0 else g.sync).dma_start(
+            T.XW[:, TC * rank + a:TC * rank + a + w], T.x[:, a:a + w]).then_inc(T.sem["x%d" % i], 16)
+
+    op("p", g.iota, (), ("II",), T.II[:], [[1, 128]], 0, 0)
+    op("p", g.iota, (), ("PI4",), T.PI4[:], [[0, 4]], 0, 1)
+    op("p", g.iota, (), ("JI",), T.JI[:], [[1, 8]], 0, 8, allow_small_or_imprecise_dtypes=True)
+    vcp(T.IH[:], T.II[:], ("II",), ("IH",))
+    vts(T.M16i[:], T.II[:], 15, None, OP.bitwise_and, R=("II",), W=("M16i",))
+    vcp(T.PJ[:, 0:1], T.PI4[:, 0:1], ("PI4",), ("PJ0",))
+    vts(T.PJ[:, 1:2], T.PI4[:, 1:2], 7, None, OP.bitwise_and, R=("PI4",), W=("PJ1",))
+    vts(T.PJ[:, 2:3], T.PI4[:, 2:3], 15, None, OP.bitwise_and, R=("PI4",), W=("PJ2",))
+    vts(T.PJ[:, 3:4], T.PI4[:, 3:4], 4, None, OP.arith_shift_right, R=("PI4",), W=("PJ3",))
+    vcp(T.M16[:], T.M16i[:], ("M16i",), ("M16",))
+    vcp(T.PC[:], T.PJ[:], ("PJ0", "PJ1", "PJ2", "PJ3"), ("PC",))
+    vts(T.on4[:], T.IH[:, 0:4], 0.0, None, OP.is_ge, R=("IH",), W=("on4",))
+    vts(T.LEs[:, 0:1], T.IH[:, 0:1], 0.0, None, OP.mult, R=("IH",), W=("LEs0",))
+    vts(T.mh[:, 0:1], T.PC[0:16, 0:1], 8.0, None, OP.is_lt, R=("PC",), W=("mh0",))
+    vts(T.mh[:, 1:2], T.PC[0:16, 0:1], 8.0, None, OP.is_ge, R=("PC",), W=("mh1",))
+    vts(T.R8[:], T.IH[0:16, 0:8], T.PC[0:16, 1:2], None, OP.is_equal, R=("IH", "PC"), W=("R8",))
+    vts(T.SL[:], T.IH[:], T.PC[:, 0:1], None, OP.is_gt, R=("IH", "PC"), W=("SL",))
+    vts(T.SU[:], T.IH[:], T.PC[:, 0:1], None, OP.is_lt, R=("IH", "PC"), W=("SU",))
+
+    for h in range(2):
+        vts(T.kl[:, h::2], T.kS[:], T.mh[:, h:h + 1], None, OP.mult, R=("kS", "mh%d" % h), W=("kl%d" % h,))
+    mm(T.psA[:, 0:8], T.kl[:], T.R8[:], ("kl0", "kl1", "R8"), ("psA",))
+    O8 = ["O%d" % t for t in range(8)]
+    for t in range(8):
+        vts(T.O[:, t::8], T.IH[:, 0:64], T.psA[:, t:t + 1], None, OP.is_equal, R=("IH", "psA"), W=(O8[t],))
+    op("v", v.tensor_tensor_scan, O8, ("S",), T.S[:], T.O[:], T.O[:], 0.0, OP.add, OP.max)
+    vcp(T.LE2[:, 0:64], T.S[:, 7::8], ("S",), ("LE2a",))
+    vcp(T.LE2[:, 64:128], T.S[:, 7::8], ("S",), ("LE2b",))
+    vcp(T.LEs[:, 1:64], T.S[:, 7:504:8], ("S",), ("LEs1",))
+    mm(T.psH[:, 0:4], T.LE2[:], T.on4[:], ("LE2a", "LE2b", "on4"), ("psH",))
+    mm(T.psB[:, 0:64], T.SL[:], T.LE2[:, 0:64], ("SL", "LE2a"), ("psB",), True, False)
+    mm(T.psB[:, 0:64], T.SU[:], T.LEs[:], ("SU", "LEs0", "LEs1"), ("psB",), False, True)
+    vcp(T.Cc[:, 4 * rank:4 * rank + 4], T.psH[:, 0:4], ("psH",), ("Cown",))
+
+    n = 0
+    for i in range(4):
+        need("p", [("x%d" % i, 16)])
+        n += send([relays[i]], inner, "XW", TC * rank + starts[i], widths[i], "xarr")
+    reads("p", ("Cown",))
+    n += send(list(idx), off, "Cc", 4 * rank, 4, "harr")
+    n += send(direct, off, "Cc", 4 * rank, 4, "harr")
+
+    for t in range(8):
+        vtt(T.SB[:, 64 * t:64 * t + 64], T.S[:, t::8], T.psB[:, 0:64], OP.add, R=("S", "psB"), W=("SB%d" % t,))
+    for t in range(8):
+        vtt(T.Wk[:, 64 * t:64 * t + 64], T.SB[:, 64 * t:64 * t + 64], T.O[:, t::8], OP.mult, R=("SB%d" % t, O8[t]), W=("Wk%d" % t,))
+    for t in range(8):
+        op("v", v.tensor_reduce, ("Wk%d" % t,), ("pos%d" % t,), T.pos[:, t:t + 1], T.Wk[:, 64 * t:64 * t + 64], AxisListType.X, OP.add)
+    vts(T.pi[:], T.pos[:], 1.0, None, OP.subtract, R=["pos%d" % t for t in range(8)], W=("pi",))
+    vts(T.hl[:, 0:8], T.pi[:], 4, None, OP.arith_shift_right, R=("pi",), W=("hl0",))
+    vts(T.hl[:, 8:16], T.pi[:], 15, None, OP.bitwise_and, R=("pi",), W=("hl1",))
+    vcp(T.hlF[:], T.hl[:], ("hl0", "hl1"), ("hlF",))
+    for t in range(8):
+        vts(T.Ah[:, 128 * t:128 * t + 128], T.M16[:], T.hlF[:, 8 + t:9 + t], None, OP.is_equal, R=("M16", "hlF"), W=("A%d" % t,))
+        vts(T.Bh[:, 64 * t:64 * t + 64], T.IH[:, 0:64], T.hlF[:, t:t + 1], T.JI[:, t:t + 1], OP.is_equal, OP.mult,
+            R=("IH", "hlF", "JI"), W=("B%d" % t,))
+        mm(T.psL[:, 0:64], T.Ah[:, 128 * t:128 * t + 128], T.Bh[:, 64 * t:64 * t + 64], ("A%d" % t, "B%d" % t), ("psL",), t == 0, t == 7)
+    vts(T.Lw[:, 64 * rank:64 * rank + 64], T.psL[:, 0:64], float(TC * rank), None, OP.add, R=("psL",), W=("Lown",))
+    reads("p", ("Lown",))
+    n += send(list(idx), off, "Lw", 64 * rank, 64, "larr")
+    n += send(direct, off, "Lw", 64 * rank, 64, "larr")
+
+    vts(T.id32[:], T.IH[:], T.PC[:, 0:1], None, OP.is_equal, R=("IH", "PC"), W=("id32",))
+    vts(T.shf[:], T.IH[:], T.PC[:, 0:1], 1.0, OP.subtract, OP.is_equal, R=("IH", "PC"), W=("shf",))
+    op("v", v.memset, (), ("shf",), T.shf[:, 64:65], 0.0)
+    vts(T.e16[:], T.M16[:], T.PC[:, 2:3], None, OP.is_equal, R=("M16", "PC"), W=("e16",))
+    vts(T.m8[:], T.IH[:, 0:8], T.PC[:, 3:4], None, OP.is_equal, R=("IH", "PC"), W=("m8",))
+    vts(T.gI[:], T.II[:], 4, None, OP.arith_shift_right, R=("II",), W=("gI",))
+    vts(sm[:, PQ:PQ + 1], T.PC[:, 0:1], float(TC * rank), None, OP.add, R=("PC",), W=("pq",))
+    vts(T.Qc[:], T.gI[:], 128.0, sm[:, PQ:PQ + 1], OP.mult, OP.add, R=("gI", "pq"), W=("Qc",))
+    vts(T.rst[:], T.M16[:], 0.0, None, OP.not_equal, R=("M16",), W=("rst",))
+    for b in range(8):
+        vts(T.i1k[:, 128 * b:128 * b + 128], T.IH[:], float(128 * b), None, OP.add, R=("IH",), W=("i1k%d" % b,))
+    op("v", v.memset, (), ("on16",), T.on16[:], 1.0)
+    vts(T.rv[:], T.i1k[:, 0:96], 0.0, 1024.0, OP.mult, OP.add, R=("i1k0",), W=("rv0", "rv1", "rv2"))
+    vts(sm[:, DR:DR + 1], T.PC[:, 0:1], 64.0, 6144.0, OP.is_ge, OP.mult, R=("PC",), W=("dr0",))
+    vts(sm[:, DR + 1:DR + 2], T.PC[:, 0:1], 0.0, 5120.0, OP.is_equal, OP.mult, R=("PC",), W=("dr1",))
+    vts(sm[:, DR:DR + 1], sm[:, DR:DR + 1], sm[:, DR + 1:DR + 2], -5120.0, OP.add, OP.add, R=("dr0", "dr1"), W=("dr0",))
+    vts(T.rv[:, 1:32:2], T.on16[:], sm[:, DR:DR + 1], None, OP.mult, R=("on16", "dr0"), W=("rv0",))
+    op("v", v.memset, (), ("PX0",), sm[:, PX:PX + 1], 0.0)
+
+    narr = 5 * _engines(off)
+    wr["Call"] = [("harr", narr)] + wr["Cown"]
+    op("v", v.tensor_tensor_scan, ("Call",), ("PX1",), sm[:, PX + 1:PX + 7], T.Cc[:, 0::4], T.Cc[:, 0::4], 0.0, OP.add, OP.max)
+    mm(T.psA[:, 0:7], T.shf[:], sm[:, PX:PX + 7], ("shf", "PX0", "PX1"), ("psA",))
+    vcp(sm[:, SH:SH + 7], T.psA[:, 0:7], ("psA",), ("ShS",))
+    vtt(sm[0:64, TG:TG + 3], sm[0:64, PX:PX + 6:2], sm[0:64, SH:SH + 6:2], OP.subtract, R=("PX0", "PX1", "ShS"), W=("tg0",))
+    vtt(sm[64:128, TG:TG + 3], sm[64:128, PX + 1:PX + 6:2], sm[64:128, SH + 1:SH + 6:2], OP.subtract, R=("PX1", "ShS"), W=("tg1",))
+    vtt(sm[:, CS:CS + 6], sm[:, SH + 1:SH + 7], sm[:, SH:SH + 6], OP.subtract, R=("ShS",), W=("CS",))
+    vts(sm[:, TH:TH + 3], sm[:, TG:TG + 3], sm[:, SH + 6:SH + 7], float(-TC * rank), OP.add, OP.add, R=("tg0", "tg1", "ShS"), W=("Th",))
+    vtt(sm[64:128, DV:DV + 3], sm[64:128, CS + 1:CS + 6:2], T.Cc[64:128, 0:17:8], OP.subtract, R=("CS", "Call"), W=("dv0",))
+    vtt(sm[0:64, DV + 1:DV + 3], sm[0:64, CS + 2:CS + 5:2], T.Cc[0:64, 4:13:8], OP.subtract, R=("CS", "Call"), W=("dv1",))
+    vtt(sm[0:64, DV:DV + 1], sm[0:64, CS:CS + 1], sm[0:64, CS + 5:CS + 6], OP.subtract, R=("CS",), W=("dv2",))
+    for s in range(3):
+        vts(T.rv[:, 32 * s:32 * s + 32:2], T.on16[:], sm[:, DV + s:DV + s + 1], None, OP.mult,
+            R=("on16", "dv0", "dv1", "dv2"), W=("rv%d" % s,))
+    for half in range(2):
+        for s in range(3):
+            a = 512 * half
+            vts(T.U[:, 1024 * s + a:1024 * s + a + 512], T.i1k[:, a:a + 512], sm[:, TH + s:TH + s + 1], None, OP.is_ge,
+                R=["i1k%d" % b for b in range(4 * half, 4 * half + 4)] + ["Th"], W=("U%d%d" % (s, half),))
+    for gr in range(8):
+        for s in range(3):
+            a = 1024 * s + 128 * gr
+            mm(T.psV[:, 32 * gr:32 * gr + 32], T.U[:, a:a + 128], T.rv[:, 32 * s:32 * s + 32],
+               ("U%d%d" % (s, gr // 4), "rv%d" % s), ("psV%d" % gr,), s == 0, s == 2)
+    PV = ["psV%d" % gr for gr in range(8)]
+    vtt(T.f1[:], T.psV[:, 0:256:2], T.Qc[:], OP.add, R=PV + ["Qc"], W=("f1",))
+    vtt(T.fi[:], T.psV[:, 1:256:2], T.f1[:], OP.add, R=PV + ["f1"], W=("fi",))
+    vts(T.hi[:], T.fi[:], 4, None, OP.arith_shift_right, R=("fi",), W=("hi",))
+    vts(T.lo[:], T.fi[:], 15, None, OP.bitwise_and, R=("fi",), W=("lo",))
+    vtt(T.hm[:], T.hi[:], T.e16[:], OP.mult, R=("hi", "e16"), W=("hm",))
+    mm(T.psO[:, 0:8], T.hm[:], T.m8[:], ("hm", "m8"), ("psO",))
+    vtt(T.lm[:], T.lo[:], T.M16i[:], OP.is_equal, R=("lo", "M16i"), W=("lm",))
+    vcp(T.off1[:], T.psO[:, 0:8], ("psO",), ("off1",))
+    wr["Lall"] = [("larr", narr)] + wr["Lown"]
+    vcp(T.G[:], T.Lw[:, 0:64 * NR].indirect(T.off1[:, 0:8]), ("Lall", "off1"), ("G",))
+    mm(T.psG[:, 0:128], T.G[:], T.id32[:], ("G", "id32"), ("psG",))
+    vtt(T.GM[:], T.psG[:, 0:128], T.lm[:], OP.mult, R=("psG", "lm"), W=("GM",))
+    op("v", v.tensor_tensor_scan, ("GM", "rst"), ("GS",), T.GS[:], T.rst[:], T.GM[:], 0.0, OP.mult, OP.add)
+    for b in range(8):
+        vts(T.lr[:, b::8], T.GS[:, 15::16], T.m8[:, b:b + 1], None, OP.mult, R=("GS", "m8"), W=("lr%d" % b,))
+    mm(T.psF[:, 0:64], T.e16[:], T.lr[:], ["e16"] + ["lr%d" % b for b in range(8)], ("psF",))
+    vcp(T.lst[:], T.psF[:, 0:64], ("psF",), ("lst",))
+
+    wr["XW"] = [("xarr", 5 * 4 * _engines(off))] + [("x%d" % i, 16) for i in range(4)]
+    for i in range(2):
+        vcp(T.yS[:, 256 * i:256 * i + 256], T.XW[:].indirect(T.lst[:, 16 * i:16 * i + 16]), ("XW", "lst"), ("y%d" % i,))
+    for i in range(2, 4):
+        op("a", g.scalar.activation, ("XW", "lst"), ("y%d" % i,), T.yS[:, 256 * i:256 * i + 256],
+           T.XW[:].indirect(T.lst[:, 16 * i:16 * i + 16]), ACT.Copy)
+    for i in range(2):
+        reads("y", ("y%d" % i,))
+        g.sync.dma_start(T.y[:, 256 * i:256 * i + 256], T.yS[:, 256 * i:256 * i + 256]).then_inc(T.sem.ysy, 16)
+    for i in range(2, 4):
+        reads("a", ("y%d" % i,))
+        g.scalar.dma_start(T.y[:, 256 * i:256 * i + 256], T.yS[:, 256 * i:256 * i + 256]).then_inc(T.sem.ysc, 16)
+    g.sync.wait_ge(T.sem.ysy, 32)
+    g.scalar.wait_ge(T.sem.ysc, 32)
+    g.wait_ge(T.sem.loc, n)
+    for s, c in cnt.items():
+        if seen.get(("p", s), 0) < c:
+            g.wait_ge(T.sem[s], c)

@@ -33,7 +33,9 @@ SCRATCH = {
 PX, SH, TG, TH, CS, DV, DR, PQ = 0, 8, 16, 20, 24, 32, 36, 40
 for _n in ("psA", "psB", "psH", "psL", "psV", "psO", "psG", "psF"):
     SCRATCH[_n] = ("psum", [128, 512], F32)
-SEMAPHORES = ["kld", "x0", "x1", "x2", "x3", "harr", "larr", "xarr", "loc", "sv", "st", "sp", "sa", "ysy", "ysc"]
+SEMAPHORES = ["kld", "x0", "x1", "x2", "x3", "harr", "larr", "xarr", "hub0", "hub1", "loc", "sv", "st", "sp", "sa", "ysy", "ysc"]
+W4 = TC // 4
+WORLD = 256
 
 
 def _engines(mask):
@@ -44,17 +46,36 @@ def _plan(T, topo, src):
     dests = [d for d in T.cores if d != src]
     direct = [d for d in dests if topo.may_write(src, d)]
     cross = [d for d in dests if not topo.may_write(src, d)]
-    first = src - src % 8
-    mine = [c for c in range(first, first + 8) if c != src and (topo.host(c), topo.chip(c)) == (topo.host(src), topo.chip(src))]
-    able = [c for c in mine if all(topo.may_write(c, d) for d in dests)]
-    near = [c for c in able if topo.die(c) == topo.die(src)]
-    far = [c for c in able if topo.die(c) != topo.die(src)]
-    relays = [c for pair in zip(near, far) for c in pair]
+    mine = [c for c in range(WORLD) if c != src and (topo.host(c), topo.chip(c)) == (topo.host(src), topo.chip(src))]
+    sides = [[c for c in mine if (topo.die(c) == topo.die(src)) == near] for near in (True, False)]
+    able = [[c for c in side if all(topo.may_write(c, d) for d in dests)] for side in sides]
     ni = (len(cross) + 1) // 2
-    widths = [192, 280, 280, 272] if ni == 1 else [192, 192, 320, 320]
-    starts = [sum(widths[:i]) for i in range(len(widths))]
-    idx = {relays[i]: cross[i::ni] for i in range(ni)}
-    return relays, starts, widths, idx, direct
+    idx = {able[i][0]: cross[i::ni] for i in range(ni)}
+    hubs_only = _crossing(T, topo, cross[0]) <= 2
+    relays = []
+    for i in range(4):
+        free = [c for c in sides[i % 2] if c not in idx and c not in relays]
+        needs_port = i < 2 and not hubs_only
+        relays.append(next(c for c in free if (c in able[i % 2]) == needs_port) if needs_port or
+                      any(c not in able[i % 2] for c in free) else free[0])
+    return relays, idx, direct
+
+
+def _crossing(T, topo, d):
+    return sum(not topo.may_write(s, d) for s in T.cores if s != d)
+
+
+def _hub(T, topo, src, i, relay, d):
+    if topo.may_write(src, d):
+        return None
+    others = [s for s in T.cores if s != d and not topo.may_write(s, d)]
+    k = others.index(src)
+    if len(others) > 2 and i < 2:
+        return None
+    hubs = [c for c in range(WORLD) if topo.mates(c, d) and topo.may_write(c, d) and topo.die(c) == topo.die(relay)]
+    if len(others) > 2:
+        return hubs[k % 2], "hub%d" % (k // 2)
+    return hubs[i // 2], "hub%d" % k
 
 
 def rank_program(g, core, T, topo):
@@ -71,29 +92,46 @@ def rank_program(g, core, T, topo):
         return _engines(mask)
 
     if rank is None:
+        n = 0
+        mates = [d for d in T.cores if topo.mates(core, d)]
+        for d in mates:
+            jobs = []
+            for r, src in enumerate(T.cores):
+                if src == d or topo.may_write(src, d):
+                    continue
+                relays = _plan(T, topo, src)[0]
+                for i in range(4):
+                    h = _hub(T, topo, src, i, relays[i], d)
+                    if h and h[0] == core:
+                        jobs.append((h[1], r, i, relays[i]))
+            for sem, r, i, relay in sorted(jobs):
+                g.wait_ge(T.sem[sem], _engines(topo.mask(relay, core)))
+                n += send([d], topo.mask(core, d), "XW", TC * r + W4 * i, W4, "xarr")
         for r, src in enumerate(T.cores):
             if (topo.host(src), topo.chip(src)) != (topo.host(core), topo.chip(core)):
                 continue
-            relays, starts, widths, idx, direct = _plan(T, topo, src)
-            if core not in relays:
-                return
-            i = relays.index(core)
-            dests = [d for d in T.cores if d != src]
-            dests = dests[i % 5:] + dests[:i % 5]
-            off = topo.mask(core, dests[0])
-            n = 0
+            relays, idx, direct = _plan(T, topo, src)
+            off = topo.mask(core, direct[0])
             if core in idx:
                 g.wait_ge(T.sem.harr, _engines(off))
                 n += send(idx[core], off, "Cc", 4 * r, 4, "harr")
-            g.wait_ge(T.sem.xarr, _engines(topo.mask(src, core) & ~topo.mask(src, direct[0])))
-            n += send(dests, off, "XW", TC * r + starts[i], widths[i], "xarr")
-            if core in idx:
                 g.wait_ge(T.sem.larr, _engines(off))
                 n += send(idx[core], off, "Lw", 64 * r, 64, "larr")
+            if core in relays:
+                i = relays.index(core)
+                far = [d for d in T.cores if d != src and d not in direct]
+                via = [_hub(T, topo, src, i, core, d) for d in far]
+                g.wait_ge(T.sem.xarr, _engines(off))
+                if via[0]:
+                    n += send([h for h, sem in via], off, "XW", TC * r + W4 * i, W4, via[0][1])
+                else:
+                    n += send(far, off, "XW", TC * r + W4 * i, W4, "xarr")
+                n += send(direct, off, "XW", TC * r + W4 * i, W4, "xarr")
+        if n:
             g.wait_ge(T.sem.loc, n)
         return
 
-    relays, starts, widths, idx, direct = _plan(T, topo, core)
+    relays, idx, direct = _plan(T, topo, core)
     off = topo.mask(core, direct[0])
     inner = topo.mask(core, relays[0]) & ~off
     eng = {"v": g.vector, "t": g.tensor, "p": g, "a": g.scalar, "y": g.sync}
@@ -147,10 +185,8 @@ def rank_program(g, core, T, topo):
 
     g.sync.dma_start(T.kS[:], T.key[:]).then_inc(T.sem.kld, 16)
     wr["kS"] = [("kld", 16)]
-    for i in range(4):
-        a, w = starts[i], widths[i]
-        (g.scalar if i % 2 == 0 else g.sync).dma_start(
-            T.XW[:, TC * rank + a:TC * rank + a + w], T.x[:, a:a + w]).then_inc(T.sem["x%d" % i], 16)
+    for i, q in ((2, g.scalar), (3, g.sync), (0, g.scalar), (1, g.sync)):
+        q.dma_start(T.XW[:, TC * rank + W4 * i:TC * rank + W4 * i + W4], T.x[:, W4 * i:W4 * i + W4]).then_inc(T.sem["x%d" % i], 16)
 
     op("p", g.iota, (), ("II",), T.II[:], [[1, 128]], 0, 0)
     op("p", g.iota, (), ("PI4",), T.PI4[:], [[0, 4]], 0, 1)
@@ -187,12 +223,13 @@ def rank_program(g, core, T, topo):
     vcp(T.Cc[:, 4 * rank:4 * rank + 4], T.psH[:, 0:4], ("psH",), ("Cown",))
 
     n = 0
-    for i in range(4):
+    for i, mask in ((2, inner), (3, inner), (0, off), (1, off)):
+        if i == 0:
+            reads("p", ("Cown",))
+            n += send(list(idx), off, "Cc", 4 * rank, 4, "harr")
+            n += send(direct, off, "Cc", 4 * rank, 4, "harr")
         need("p", [("x%d" % i, 16)])
-        n += send([relays[i]], inner, "XW", TC * rank + starts[i], widths[i], "xarr")
-    reads("p", ("Cown",))
-    n += send(list(idx), off, "Cc", 4 * rank, 4, "harr")
-    n += send(direct, off, "Cc", 4 * rank, 4, "harr")
+        n += send([relays[i]], mask, "XW", TC * rank + W4 * i, W4, "xarr")
 
     for t in range(8):
         vtt(T.SB[:, 64 * t:64 * t + 64], T.S[:, t::8], T.psB[:, 0:64], OP.add, R=("S", "psB"), W=("SB%d" % t,))

@@ -14,27 +14,30 @@ SCRATCH = {
     "JI": ("sbuf", [128, 8], F32), "PC": ("sbuf", [128, 4], F32), "IH": ("sbuf", [128, 128], F16),
     "M16i": ("sbuf", [128, 128], I32), "M16": ("sbuf", [128, 128], F16), "mh": ("sbuf", [16, 2], F32),
     "R8": ("sbuf", [16, 8], F16), "SL": ("sbuf", [128, 128], F16), "SU": ("sbuf", [128, 128], F16),
-    "on4": ("sbuf", [128, 4], F16), "kl": ("sbuf", [16, 128], F16), "O": ("sbuf", [128, 512], F16),
+    "h16": ("sbuf", [128, 16], F16),
+    "kl": ("sbuf", [16, 128], F16), "O": ("sbuf", [128, 512], F16),
     "S": ("sbuf", [128, 512], F16), "LE2": ("sbuf", [128, 128], F16), "LEs": ("sbuf", [128, 64], F16),
-    "SB": ("sbuf", [128, 512], F16), "Wk": ("sbuf", [128, 512], F16), "pos": ("sbuf", [128, 8], F32),
+    "SB": ("sbuf", [128, 512], F16), "Wk": ("sbuf", [128, 512], F32), "pos": ("sbuf", [128, 8], F32),
     "pi": ("sbuf", [128, 8], I32), "hl": ("sbuf", [128, 16], I32), "hlF": ("sbuf", [128, 16], F32),
     "Ah": ("sbuf", [128, 1024], F16), "Bh": ("sbuf", [128, 512], F16),
-    "id32": ("sbuf", [128, 128], F32), "shf": ("sbuf", [128, 128], F32), "e16": ("sbuf", [128, 128], F32),
+    "id16": ("sbuf", [128, 128], F16), "shf": ("sbuf", [128, 128], F32), "e16": ("sbuf", [128, 128], F16),
     "m8": ("sbuf", [128, 8], F32), "gI": ("sbuf", [128, 128], I32),
-    "Qc": ("sbuf", [128, 128], F32), "rst": ("sbuf", [128, 128], F32), "i1k": ("sbuf", [128, 1024], F16),
+    "Qc": ("sbuf", [128, 128], F32), "rst": ("sbuf", [128, 128], F16), "i1k": ("sbuf", [128, 1024], F16),
     "on16": ("sbuf", [128, 16], F32), "rv": ("sbuf", [128, 96], F16),
     "sm": ("sbuf", [128, 48], F32),
     "U": ("sbuf", [128, 3 * 1024], F16), "f1": ("sbuf", [128, 128], F32), "fi": ("sbuf", [128, 128], I32),
-    "hi": ("sbuf", [128, 128], I32), "lo": ("sbuf", [128, 128], I32), "hm": ("sbuf", [128, 128], F32),
-    "lm": ("sbuf", [128, 128], F32), "off1": ("sbuf", [128, 8], U16), "G": ("sbuf", [128, 128], F32),
-    "GM": ("sbuf", [128, 128], F32), "GS": ("sbuf", [128, 128], F32), "lr": ("sbuf", [128, 64], F32),
+    "hi": ("sbuf", [128, 128], I32), "lo": ("sbuf", [128, 128], I32), "hm": ("sbuf", [128, 128], F16),
+    "lm": ("sbuf", [128, 128], F16), "off1": ("sbuf", [128, 8], U16), "G": ("sbuf", [128, 128], F16),
+    "GM": ("sbuf", [128, 128], F16), "GS": ("sbuf", [128, 128], F16), "lr": ("sbuf", [128, 128], F16),
     "lst": ("sbuf", [128, 64], U16),
 }
 PX, SH, TG, TH, CS, DV, DR, PQ = 0, 8, 16, 20, 24, 32, 36, 40
 for _n in ("psA", "psB", "psH", "psL", "psV", "psO", "psG", "psF"):
     SCRATCH[_n] = ("psum", [128, 512], F32)
-SEMAPHORES = ["kld", "x0", "x1", "x2", "x3", "harr", "larr", "xarr", "hub0", "hub1", "loc", "sv", "st", "sp", "sa", "ysy", "ysc"]
-W4 = TC // 4
+SEMAPHORES = ["kld", "x0", "x1", "x2", "harr", "larr", "xarr", "hub0", "hub1", "hub2", "hub3", "loc", "sv", "st", "sp", "sa",
+              "ysy", "ysc"]
+WID = [172, 172, 172, 172, 168, 168]
+BEG = [sum(WID[:i]) for i in range(7)]
 WORLD = 256
 
 
@@ -47,35 +50,25 @@ def _plan(T, topo, src):
     direct = [d for d in dests if topo.may_write(src, d)]
     cross = [d for d in dests if not topo.may_write(src, d)]
     mine = [c for c in range(WORLD) if c != src and (topo.host(c), topo.chip(c)) == (topo.host(src), topo.chip(src))]
-    sides = [[c for c in mine if (topo.die(c) == topo.die(src)) == near] for near in (True, False)]
-    able = [[c for c in side if all(topo.may_write(c, d) for d in dests)] for side in sides]
-    ni = (len(cross) + 1) // 2
-    idx = {able[i][0]: cross[i::ni] for i in range(ni)}
-    hubs_only = _crossing(T, topo, cross[0]) <= 2
-    relays = []
-    for i in range(4):
-        free = [c for c in sides[i % 2] if c not in idx and c not in relays]
-        needs_port = i < 2 and not hubs_only
-        relays.append(next(c for c in free if (c in able[i % 2]) == needs_port) if needs_port or
-                      any(c not in able[i % 2] for c in free) else free[0])
-    return relays, idx, direct
-
-
-def _crossing(T, topo, d):
-    return sum(not topo.may_write(s, d) for s in T.cores if s != d)
+    able = [c for c in mine if all(topo.may_write(c, d) for d in dests)]
+    idx = [c for c in able if topo.die(c) != topo.die(src)][-1]
+    sides = [[c for c in mine if c != idx and (topo.die(c) == topo.die(src)) == near] for near in (True, False)]
+    sides = [sorted(side, key=lambda c: (c in able, c))[:3] for side in sides]
+    relays = [sides[i % 2][i // 2] for i in range(6)]
+    return relays, idx, cross, direct
 
 
 def _hub(T, topo, src, i, relay, d):
     if topo.may_write(src, d):
         return None
     others = [s for s in T.cores if s != d and not topo.may_write(s, d)]
-    k = others.index(src)
-    if len(others) > 2 and i < 2:
+    k, j = others.index(src), i // 2
+    if len(others) > 2 and i >= 4:
         return None
     hubs = [c for c in range(WORLD) if topo.mates(c, d) and topo.may_write(c, d) and topo.die(c) == topo.die(relay)]
     if len(others) > 2:
-        return hubs[k % 2], "hub%d" % (k // 2)
-    return hubs[i // 2], "hub%d" % k
+        return hubs[j], "hub%d" % k
+    return hubs[(j + k) % 2], "hub%d" % j
 
 
 def rank_program(g, core, T, topo):
@@ -93,45 +86,43 @@ def rank_program(g, core, T, topo):
 
     if rank is None:
         n = 0
-        mates = [d for d in T.cores if topo.mates(core, d)]
-        for d in mates:
+        for d in [d for d in T.cores if topo.mates(core, d)]:
             jobs = []
             for r, src in enumerate(T.cores):
                 if src == d or topo.may_write(src, d):
                     continue
                 relays = _plan(T, topo, src)[0]
-                for i in range(4):
+                for i in range(6):
                     h = _hub(T, topo, src, i, relays[i], d)
                     if h and h[0] == core:
                         jobs.append((h[1], r, i, relays[i]))
             for sem, r, i, relay in sorted(jobs):
                 g.wait_ge(T.sem[sem], _engines(topo.mask(relay, core)))
-                n += send([d], topo.mask(core, d), "XW", TC * r + W4 * i, W4, "xarr")
+                n += send([d], topo.mask(core, d), "XW", TC * r + BEG[i], WID[i], "xarr")
         for r, src in enumerate(T.cores):
             if (topo.host(src), topo.chip(src)) != (topo.host(core), topo.chip(core)):
                 continue
-            relays, idx, direct = _plan(T, topo, src)
+            relays, idx, cross, direct = _plan(T, topo, src)
             off = topo.mask(core, direct[0])
-            if core in idx:
+            if core == idx:
                 g.wait_ge(T.sem.harr, _engines(off))
-                n += send(idx[core], off, "Cc", 4 * r, 4, "harr")
+                n += send(cross, off, "Cc", 4 * r, 4, "harr")
                 g.wait_ge(T.sem.larr, _engines(off))
-                n += send(idx[core], off, "Lw", 64 * r, 64, "larr")
+                n += send(cross, off, "Lw", 64 * r, 64, "larr")
             if core in relays:
                 i = relays.index(core)
-                far = [d for d in T.cores if d != src and d not in direct]
-                via = [_hub(T, topo, src, i, core, d) for d in far]
+                via = [_hub(T, topo, src, i, core, d) for d in cross]
                 g.wait_ge(T.sem.xarr, _engines(off))
                 if via[0]:
-                    n += send([h for h, sem in via], off, "XW", TC * r + W4 * i, W4, via[0][1])
+                    n += send([h for h, sem in via], off, "XW", TC * r + BEG[i], WID[i], via[0][1])
                 else:
-                    n += send(far, off, "XW", TC * r + W4 * i, W4, "xarr")
-                n += send(direct, off, "XW", TC * r + W4 * i, W4, "xarr")
+                    n += send(cross, off, "XW", TC * r + BEG[i], WID[i], "xarr")
+                n += send(direct, off, "XW", TC * r + BEG[i], WID[i], "xarr")
         if n:
             g.wait_ge(T.sem.loc, n)
         return
 
-    relays, idx, direct = _plan(T, topo, core)
+    relays, idx, cross, direct = _plan(T, topo, core)
     off = topo.mask(core, direct[0])
     inner = topo.mask(core, relays[0]) & ~off
     eng = {"v": g.vector, "t": g.tensor, "p": g, "a": g.scalar, "y": g.sync}
@@ -185,8 +176,9 @@ def rank_program(g, core, T, topo):
 
     g.sync.dma_start(T.kS[:], T.key[:]).then_inc(T.sem.kld, 16)
     wr["kS"] = [("kld", 16)]
-    for i, q in ((2, g.scalar), (3, g.sync), (0, g.scalar), (1, g.sync)):
-        q.dma_start(T.XW[:, TC * rank + W4 * i:TC * rank + W4 * i + W4], T.x[:, W4 * i:W4 * i + W4]).then_inc(T.sem["x%d" % i], 16)
+    for i, q in enumerate((g.scalar, g.sync, g.scalar)):
+        a, b = BEG[2 * i], BEG[2 * i + 2]
+        q.dma_start(T.XW[:, TC * rank + a:TC * rank + b], T.x[:, a:b]).then_inc(T.sem["x%d" % i], 16)
 
     op("p", g.iota, (), ("II",), T.II[:], [[1, 128]], 0, 0)
     op("p", g.iota, (), ("PI4",), T.PI4[:], [[0, 4]], 0, 1)
@@ -199,7 +191,7 @@ def rank_program(g, core, T, topo):
     vts(T.PJ[:, 3:4], T.PI4[:, 3:4], 4, None, OP.arith_shift_right, R=("PI4",), W=("PJ3",))
     vcp(T.M16[:], T.M16i[:], ("M16i",), ("M16",))
     vcp(T.PC[:], T.PJ[:], ("PJ0", "PJ1", "PJ2", "PJ3"), ("PC",))
-    vts(T.on4[:], T.IH[:, 0:4], 0.0, None, OP.is_ge, R=("IH",), W=("on4",))
+    vts(T.h16[:, 0:4], T.IH[:, 0:4], 0.0, None, OP.is_ge, R=("IH",), W=("on4",))
     vts(T.LEs[:, 0:1], T.IH[:, 0:1], 0.0, None, OP.mult, R=("IH",), W=("LEs0",))
     vts(T.mh[:, 0:1], T.PC[0:16, 0:1], 8.0, None, OP.is_lt, R=("PC",), W=("mh0",))
     vts(T.mh[:, 1:2], T.PC[0:16, 0:1], 8.0, None, OP.is_ge, R=("PC",), W=("mh1",))
@@ -217,26 +209,29 @@ def rank_program(g, core, T, topo):
     vcp(T.LE2[:, 0:64], T.S[:, 7::8], ("S",), ("LE2a",))
     vcp(T.LE2[:, 64:128], T.S[:, 7::8], ("S",), ("LE2b",))
     vcp(T.LEs[:, 1:64], T.S[:, 7:504:8], ("S",), ("LEs1",))
-    mm(T.psH[:, 0:4], T.LE2[:], T.on4[:], ("LE2a", "LE2b", "on4"), ("psH",))
+    mm(T.psH[:, 0:4], T.LE2[:], T.h16[:, 0:4], ("LE2a", "LE2b", "on4"), ("psH",))
     mm(T.psB[:, 0:64], T.SL[:], T.LE2[:, 0:64], ("SL", "LE2a"), ("psB",), True, False)
     mm(T.psB[:, 0:64], T.SU[:], T.LEs[:], ("SU", "LEs0", "LEs1"), ("psB",), False, True)
     vcp(T.Cc[:, 4 * rank:4 * rank + 4], T.psH[:, 0:4], ("psH",), ("Cown",))
 
     n = 0
-    for i, mask in ((2, inner), (3, inner), (0, off), (1, off)):
-        if i == 0:
+    for i in range(6):
+        if i == 3:
             reads("p", ("Cown",))
-            n += send(list(idx), off, "Cc", 4 * rank, 4, "harr")
+            n += send([idx], off, "Cc", 4 * rank, 4, "harr")
             n += send(direct, off, "Cc", 4 * rank, 4, "harr")
-        need("p", [("x%d" % i, 16)])
-        n += send([relays[i]], mask, "XW", TC * rank + W4 * i, W4, "xarr")
+        need("p", [("x%d" % (i // 2), 16)])
+        n += send([relays[i]], inner if i < 3 else off, "XW", TC * rank + BEG[i], WID[i], "xarr")
 
     for t in range(8):
         vtt(T.SB[:, 64 * t:64 * t + 64], T.S[:, t::8], T.psB[:, 0:64], OP.add, R=("S", "psB"), W=("SB%d" % t,))
-    for t in range(8):
+    for t in (4, 5, 6, 7, 0, 1, 2, 3):
         vtt(T.Wk[:, 64 * t:64 * t + 64], T.SB[:, 64 * t:64 * t + 64], T.O[:, t::8], OP.mult, R=("SB%d" % t, O8[t]), W=("Wk%d" % t,))
-    for t in range(8):
+    for t in range(4):
         op("v", v.tensor_reduce, ("Wk%d" % t,), ("pos%d" % t,), T.pos[:, t:t + 1], T.Wk[:, 64 * t:64 * t + 64], AxisListType.X, OP.add)
+    for t in range(4, 8):
+        op("a", g.scalar.activation, ("Wk%d" % t,), ("pos%d" % t,), T.yS[:, 64 * t:64 * t + 64], T.Wk[:, 64 * t:64 * t + 64],
+           ACT.Copy, accum_out=T.pos[:, t:t + 1])
     vts(T.pi[:], T.pos[:], 1.0, None, OP.subtract, R=["pos%d" % t for t in range(8)], W=("pi",))
     vts(T.hl[:, 0:8], T.pi[:], 4, None, OP.arith_shift_right, R=("pi",), W=("hl0",))
     vts(T.hl[:, 8:16], T.pi[:], 15, None, OP.bitwise_and, R=("pi",), W=("hl1",))
@@ -246,20 +241,13 @@ def rank_program(g, core, T, topo):
         vts(T.Bh[:, 64 * t:64 * t + 64], T.IH[:, 0:64], T.hlF[:, t:t + 1], T.JI[:, t:t + 1], OP.is_equal, OP.mult,
             R=("IH", "hlF", "JI"), W=("B%d" % t,))
         mm(T.psL[:, 0:64], T.Ah[:, 128 * t:128 * t + 128], T.Bh[:, 64 * t:64 * t + 64], ("A%d" % t, "B%d" % t), ("psL",), t == 0, t == 7)
-    vts(T.Lw[:, 64 * rank:64 * rank + 64], T.psL[:, 0:64], float(TC * rank), None, OP.add, R=("psL",), W=("Lown",))
+    vcp(T.Lw[:, 64 * rank:64 * rank + 64], T.psL[:, 0:64], ("psL",), ("Lown",))
     reads("p", ("Lown",))
-    n += send(list(idx), off, "Lw", 64 * rank, 64, "larr")
+    n += send([idx], off, "Lw", 64 * rank, 64, "larr")
     n += send(direct, off, "Lw", 64 * rank, 64, "larr")
 
-    vts(T.id32[:], T.IH[:], T.PC[:, 0:1], None, OP.is_equal, R=("IH", "PC"), W=("id32",))
     vts(T.shf[:], T.IH[:], T.PC[:, 0:1], 1.0, OP.subtract, OP.is_equal, R=("IH", "PC"), W=("shf",))
     op("v", v.memset, (), ("shf",), T.shf[:, 64:65], 0.0)
-    vts(T.e16[:], T.M16[:], T.PC[:, 2:3], None, OP.is_equal, R=("M16", "PC"), W=("e16",))
-    vts(T.m8[:], T.IH[:, 0:8], T.PC[:, 3:4], None, OP.is_equal, R=("IH", "PC"), W=("m8",))
-    vts(T.gI[:], T.II[:], 4, None, OP.arith_shift_right, R=("II",), W=("gI",))
-    vts(sm[:, PQ:PQ + 1], T.PC[:, 0:1], float(TC * rank), None, OP.add, R=("PC",), W=("pq",))
-    vts(T.Qc[:], T.gI[:], 128.0, sm[:, PQ:PQ + 1], OP.mult, OP.add, R=("gI", "pq"), W=("Qc",))
-    vts(T.rst[:], T.M16[:], 0.0, None, OP.not_equal, R=("M16",), W=("rst",))
     for b in range(8):
         vts(T.i1k[:, 128 * b:128 * b + 128], T.IH[:], float(128 * b), None, OP.add, R=("IH",), W=("i1k%d" % b,))
     op("v", v.memset, (), ("on16",), T.on16[:], 1.0)
@@ -269,6 +257,14 @@ def rank_program(g, core, T, topo):
     vts(sm[:, DR:DR + 1], sm[:, DR:DR + 1], sm[:, DR + 1:DR + 2], -5120.0, OP.add, OP.add, R=("dr0", "dr1"), W=("dr0",))
     vts(T.rv[:, 1:32:2], T.on16[:], sm[:, DR:DR + 1], None, OP.mult, R=("on16", "dr0"), W=("rv0",))
     op("v", v.memset, (), ("PX0",), sm[:, PX:PX + 1], 0.0)
+    vts(T.gI[:], T.II[:], 4, None, OP.arith_shift_right, R=("II",), W=("gI",))
+    vts(sm[:, PQ:PQ + 1], T.PC[:, 0:1], float(TC * rank), None, OP.add, R=("PC",), W=("pq",))
+    vts(T.Qc[:], T.gI[:], 128.0, sm[:, PQ:PQ + 1], OP.mult, OP.add, R=("gI", "pq"), W=("Qc",))
+    vts(T.e16[:], T.M16[:], T.PC[:, 2:3], None, OP.is_equal, R=("M16", "PC"), W=("e16",))
+    vts(T.m8[:], T.IH[:, 0:8], T.PC[:, 3:4], None, OP.is_equal, R=("IH", "PC"), W=("m8",))
+    vcp(T.h16[:, 8:16], T.m8[:], ("m8",), ("m8h",))
+    vts(T.id16[:], T.IH[:], T.PC[:, 0:1], None, OP.is_equal, R=("IH", "PC"), W=("id16",))
+    vts(T.rst[:], T.M16[:], 0.0, None, OP.not_equal, R=("M16",), W=("rst",))
 
     narr = 5 * _engines(off)
     wr["Call"] = [("harr", narr)] + wr["Cown"]
@@ -285,36 +281,39 @@ def rank_program(g, core, T, topo):
     for s in range(3):
         vts(T.rv[:, 32 * s:32 * s + 32:2], T.on16[:], sm[:, DV + s:DV + s + 1], None, OP.mult,
             R=("on16", "dv0", "dv1", "dv2"), W=("rv%d" % s,))
-    for half in range(2):
+    for part in range(4):
         for s in range(3):
-            a = 512 * half
-            vts(T.U[:, 1024 * s + a:1024 * s + a + 512], T.i1k[:, a:a + 512], sm[:, TH + s:TH + s + 1], None, OP.is_ge,
-                R=["i1k%d" % b for b in range(4 * half, 4 * half + 4)] + ["Th"], W=("U%d%d" % (s, half),))
+            a = 256 * part
+            vts(T.U[:, 1024 * s + a:1024 * s + a + 256], T.i1k[:, a:a + 256], sm[:, TH + s:TH + s + 1], None, OP.is_ge,
+                R=("i1k%d" % (2 * part), "i1k%d" % (2 * part + 1), "Th"), W=("U%d%d" % (s, part),))
     for gr in range(8):
         for s in range(3):
             a = 1024 * s + 128 * gr
             mm(T.psV[:, 32 * gr:32 * gr + 32], T.U[:, a:a + 128], T.rv[:, 32 * s:32 * s + 32],
-               ("U%d%d" % (s, gr // 4), "rv%d" % s), ("psV%d" % gr,), s == 0, s == 2)
+               ("U%d%d" % (s, gr // 2), "rv%d" % s), ("psV%d" % gr,), s == 0, s == 2)
     PV = ["psV%d" % gr for gr in range(8)]
     vtt(T.f1[:], T.psV[:, 0:256:2], T.Qc[:], OP.add, R=PV + ["Qc"], W=("f1",))
     vtt(T.fi[:], T.psV[:, 1:256:2], T.f1[:], OP.add, R=PV + ["f1"], W=("fi",))
     vts(T.hi[:], T.fi[:], 4, None, OP.arith_shift_right, R=("fi",), W=("hi",))
     vts(T.lo[:], T.fi[:], 15, None, OP.bitwise_and, R=("fi",), W=("lo",))
     vtt(T.hm[:], T.hi[:], T.e16[:], OP.mult, R=("hi", "e16"), W=("hm",))
-    mm(T.psO[:, 0:8], T.hm[:], T.m8[:], ("hm", "m8"), ("psO",))
+    mm(T.psO[:, 0:8], T.hm[:], T.h16[:, 8:16], ("hm", "m8h"), ("psO",))
     vtt(T.lm[:], T.lo[:], T.M16i[:], OP.is_equal, R=("lo", "M16i"), W=("lm",))
     vcp(T.off1[:], T.psO[:, 0:8], ("psO",), ("off1",))
     wr["Lall"] = [("larr", narr)] + wr["Lown"]
     vcp(T.G[:], T.Lw[:, 0:64 * NR].indirect(T.off1[:, 0:8]), ("Lall", "off1"), ("G",))
-    mm(T.psG[:, 0:128], T.G[:], T.id32[:], ("G", "id32"), ("psG",))
+    mm(T.psG[:, 0:128], T.G[:], T.id16[:], ("G", "id16"), ("psG",))
+    for b in range(8):
+        vts(T.lr[:, 64 + b::8], T.psV[:, 1:256:32], T.m8[:, b:b + 1], None, OP.mult, R=PV + ["m8"], W=("lrR%d" % b,))
     vtt(T.GM[:], T.psG[:, 0:128], T.lm[:], OP.mult, R=("psG", "lm"), W=("GM",))
     op("v", v.tensor_tensor_scan, ("GM", "rst"), ("GS",), T.GS[:], T.rst[:], T.GM[:], 0.0, OP.mult, OP.add)
+    mm(T.psF[:, 0:64], T.e16[:], T.lr[:, 64:128], ["e16"] + ["lrR%d" % b for b in range(8)], ("psF",), True, False)
     for b in range(8):
-        vts(T.lr[:, b::8], T.GS[:, 15::16], T.m8[:, b:b + 1], None, OP.mult, R=("GS", "m8"), W=("lr%d" % b,))
-    mm(T.psF[:, 0:64], T.e16[:], T.lr[:], ["e16"] + ["lr%d" % b for b in range(8)], ("psF",))
+        vts(T.lr[:, b:64:8], T.GS[:, 15::16], T.m8[:, b:b + 1], None, OP.mult, R=("GS", "m8"), W=("lr%d" % b,))
+    mm(T.psF[:, 0:64], T.e16[:], T.lr[:, 0:64], ["e16"] + ["lr%d" % b for b in range(8)], ("psF",), False, True)
     vcp(T.lst[:], T.psF[:, 0:64], ("psF",), ("lst",))
 
-    wr["XW"] = [("xarr", 5 * 4 * _engines(off))] + [("x%d" % i, 16) for i in range(4)]
+    wr["XW"] = [("xarr", 5 * 6 * _engines(off))] + [("x%d" % i, 16) for i in range(3)]
     for i in range(2):
         vcp(T.yS[:, 256 * i:256 * i + 256], T.XW[:].indirect(T.lst[:, 16 * i:16 * i + 16]), ("XW", "lst"), ("y%d" % i,))
     for i in range(2, 4):

from concourse.bass import DstId, RemoteDMATransfer
from concourse.mybir import AluOpType as OP, AxisListType, ActivationFunctionType as ACT

NR, TC, NK = 6, 1024, 64
F32, F16, I32, U16 = "float32", "float16", "int32", "uint16"

SCRATCH = {
    "XW": ("sbuf", [128, NR * TC], F32),
    "yS": ("sbuf", [128, TC], F32),
    "Lw": ("sbuf", [128, NR * 64], F32),
    "Cc": ("sbuf", [128, NR * 4], F32),
    "kS": ("sbuf", [16, 64], I32),
    "II": ("sbuf", [128, 128], I32), "PI4": ("sbuf", [128, 4], I32), "PJ": ("sbuf", [128, 4], I32),
    "JI": ("sbuf", [128, 8], F32), "PC": ("sbuf", [128, 4], F32), "IH": ("sbuf", [128, 128], F16),
    "M16i": ("sbuf", [128, 128], I32), "M16": ("sbuf", [128, 128], F16), "mh": ("sbuf", [16, 2], F32),
    "R8": ("sbuf", [16, 8], F16), "SL": ("sbuf", [128, 128], F16), "SU": ("sbuf", [128, 128], F16),
    "h16": ("sbuf", [128, 16], F16),
    "kl": ("sbuf", [16, 128], F16), "O": ("sbuf", [128, 512], F16),
    "S": ("sbuf", [128, 512], F16), "LE2": ("sbuf", [128, 128], F16), "LEs": ("sbuf", [128, 64], F16),
    "SB": ("sbuf", [128, 512], F16), "Wk": ("sbuf", [128, 512], F32), "pos": ("sbuf", [128, 8], F32),
    "pi": ("sbuf", [128, 8], I32), "hl": ("sbuf", [128, 16], I32), "hlF": ("sbuf", [128, 16], F32),
    "Ah": ("sbuf", [128, 1024], F16), "Bh": ("sbuf", [128, 512], F16),
    "id16": ("sbuf", [128, 128], F16), "shf": ("sbuf", [128, 128], F32), "e16": ("sbuf", [128, 128], F16),
    "m8": ("sbuf", [128, 8], F32), "gI": ("sbuf", [128, 128], I32),
    "Qc": ("sbuf", [128, 128], F32), "rst": ("sbuf", [128, 128], F16), "i1k": ("sbuf", [128, 1024], F16),
    "on16": ("sbuf", [128, 16], F32), "rv": ("sbuf", [128, 96], F16),
    "sm": ("sbuf", [128, 48], F32),
    "U": ("sbuf", [128, 3 * 1024], F16), "f1": ("sbuf", [128, 128], F32), "fi": ("sbuf", [128, 128], I32),
    "hi": ("sbuf", [128, 128], I32), "lo": ("sbuf", [128, 128], I32), "hm": ("sbuf", [128, 128], F16),
    "lm": ("sbuf", [128, 128], F16), "off1": ("sbuf", [128, 8], U16), "G": ("sbuf", [128, 128], F16),
    "GM": ("sbuf", [128, 128], F16), "GS": ("sbuf", [128, 128], F16), "lr": ("sbuf", [128, 128], F16),
    "lst": ("sbuf", [128, 64], U16),
}
PX, SH, TG, TH, CS, DV, DR, PQ = 0, 8, 16, 20, 24, 32, 36, 40
for _n in ("psA", "psB", "psH", "psL", "psV", "psO", "psG", "psF"):
    SCRATCH[_n] = ("psum", [128, 512], F32)
SEMAPHORES = ["kld", "x0", "x1", "x2", "harr", "larr", "xarr", "hub0", "hub1", "hub2", "hub3", "loc", "sv", "st", "sp", "sa",
              "ysy", "ysc"]
WID = [172, 172, 172, 172, 168, 168]
BEG = [sum(WID[:i]) for i in range(7)]
WORLD = 256


def _engines(mask):
    return bin(mask).count("1")


def _plan(T, topo, src):
    dests = [d for d in T.cores if d != src]
    direct = [d for d in dests if topo.may_write(src, d)]
    cross = [d for d in dests if not topo.may_write(src, d)]
    mine = [c for c in range(WORLD) if c != src and (topo.host(c), topo.chip(c)) == (topo.host(src), topo.chip(src))]
    able = [c for c in mine if all(topo.may_write(c, d) for d in dests)]
    idx = [c for c in able if topo.die(c) != topo.die(src)][-1]
    sides = [[c for c in mine if c != idx and (topo.die(c) == topo.die(src)) == near] for near in (True, False)]
    sides = [sorted(side, key=lambda c: (c in able, c))[:3] for side in sides]
    relays = [sides[i % 2][i // 2] for i in range(6)]
    return relays, idx, cross, direct


def _hub(T, topo, src, i, relay, d):
    if topo.may_write(src, d):
        return None
    others = [s for s in T.cores if s != d and not topo.may_write(s, d)]
    k, j = others.index(src), i // 2
    if len(others) > 2 and i >= 4:
        return None
    hubs = [c for c in range(WORLD) if topo.mates(c, d) and topo.may_write(c, d) and topo.die(c) == topo.die(relay)]
    if len(others) > 2:
        return hubs[j], "hub%d" % k
    return hubs[(j + k) % 2], "hub%d" % j


def rank_program(g, core, T, topo):
    rank = T.rank_of(core)

    def send(dests, mask, name, a, w, rsem):
        ids = []
        for d in dests:
            rid, pnc = topo.addr(d, core)
            ids.append(DstId(rid=rid, pnc=pnc))
        ap = T[name][:, a:a + w]
        g.remote_dma_fused([RemoteDMATransfer(dst_ids=ids, dma_engine_mask=mask, remote_sem=T.sem[rsem],
                                              srcs=[ap], dsts=[ap for d in dests])], local_sem=T.sem.loc)
        return _engines(mask)

    if rank is None:
        n = 0
        for d in [d for d in T.cores if topo.mates(core, d)]:
            jobs = []
            for r, src in enumerate(T.cores):
                if src == d or topo.may_write(src, d):
                    continue
                relays = _plan(T, topo, src)[0]
                for i in range(6):
                    h = _hub(T, topo, src, i, relays[i], d)
                    if h and h[0] == core:
                        jobs.append((h[1], r, i, relays[i]))
            for sem, r, i, relay in sorted(jobs):
                g.wait_ge(T.sem[sem], _engines(topo.mask(relay, core)))
                n += send([d], topo.mask(core, d), "XW", TC * r + BEG[i], WID[i], "xarr")
        for r, src in enumerate(T.cores):
            if (topo.host(src), topo.chip(src)) != (topo.host(core), topo.chip(core)):
                continue
            relays, idx, cross, direct = _plan(T, topo, src)
            off = topo.mask(core, direct[0])
            if core == idx:
                g.wait_ge(T.sem.harr, _engines(off))
                n += send(cross, off, "Cc", 4 * r, 4, "harr")
                g.wait_ge(T.sem.larr, _engines(off))
                n += send(cross, off, "Lw", 64 * r, 64, "larr")
            if core in relays:
                i = relays.index(core)
                via = [_hub(T, topo, src, i, core, d) for d in cross]
                g.wait_ge(T.sem.xarr, _engines(off))
                if via[0]:
                    n += send([h for h, sem in via], off, "XW", TC * r + BEG[i], WID[i], via[0][1])
                else:
                    n += send(cross, off, "XW", TC * r + BEG[i], WID[i], "xarr")
                n += send(direct, off, "XW", TC * r + BEG[i], WID[i], "xarr")
        if n:
            g.wait_ge(T.sem.loc, n)
        return

    relays, idx, cross, direct = _plan(T, topo, core)
    off = topo.mask(core, direct[0])
    inner = topo.mask(core, relays[0]) & ~off
    eng = {"v": g.vector, "t": g.tensor, "p": g, "a": g.scalar, "y": g.sync}
    semof = {"v": "sv", "t": "st", "p": "sp", "a": "sa"}
    cnt, seen, wr, rd = {}, {}, {}, {}

    def need(q, toks):
        best = {}
        for s, n in toks:
            best[s] = max(best.get(s, 0), n)
        for s, n in best.items():
            if seen.get((q, s), 0) < n:
                eng[q].wait_ge(T.sem[s], n)
                seen[(q, s)] = n

    def reads(q, names):
        need(q, [t for n in names for t in wr.get(n, [])])

    def op(q, fn, rds, wrs, *args, inc=True, **kw):
        toks = [t for n in rds for t in wr.get(n, [])]
        for n in wrs:
            toks += wr.get(n, []) + rd.get(n, [])
        need(q, toks)
        ins = fn(*args, **kw)
        if inc:
            s = semof[q]
            ins.then_inc(T.sem[s], 1)
            cnt[s] = cnt.get(s, 0) + 1
            for n in rds:
                rd.setdefault(n, []).append((s, cnt[s]))
            for n in wrs:
                wr[n] = [(s, cnt[s])]
                rd[n] = []

    v, t_, sm = g.vector, g.tensor, T.sm

    def vts(o, i, s1, s2, o0, o1=None, R=(), W=()):
        if o1 is None:
            op("v", v.tensor_scalar, R, W, o, i, s1, s2, o0)
        else:
            op("v", v.tensor_scalar, R, W, o, i, s1, s2, o0, o1)

    def vtt(o, a, b, o0, R=(), W=()):
        op("v", v.tensor_tensor, R, W, o, a, b, o0)

    def vcp(o, i, R=(), W=()):
        op("v", v.tensor_copy, R, W, o, i)

    def mm(o, l, r, R, W, start=True, stop=True):
        op("t", t_.matmul, R, W if stop else (), o, l, r, start, stop, inc=stop)

    g.sync.dma_start(T.kS[:], T.key[:]).then_inc(T.sem.kld, 16)
    wr["kS"] = [("kld", 16)]
    for i, q in enumerate((g.scalar, g.sync, g.scalar)):
        a, b = BEG[2 * i], BEG[2 * i + 2]
        q.dma_start(T.XW[:, TC * rank + a:TC * rank + b], T.x[:, a:b]).then_inc(T.sem["x%d" % i], 16)

    op("p", g.iota, (), ("II",), T.II[:], [[1, 128]], 0, 0)
    op("p", g.iota, (), ("PI4",), T.PI4[:], [[0, 4]], 0, 1)
    op("p", g.iota, (), ("JI",), T.JI[:], [[1, 8]], 0, 8, allow_small_or_imprecise_dtypes=True)
    vcp(T.IH[:], T.II[:], ("II",), ("IH",))
    vts(T.M16i[:], T.II[:], 15, None, OP.bitwise_and, R=("II",), W=("M16i",))
    vcp(T.PJ[:, 0:1], T.PI4[:, 0:1], ("PI4",), ("PJ0",))
    vts(T.PJ[:, 1:2], T.PI4[:, 1:2], 7, None, OP.bitwise_and, R=("PI4",), W=("PJ1",))
    vts(T.PJ[:, 2:3], T.PI4[:, 2:3], 15, None, OP.bitwise_and, R=("PI4",), W=("PJ2",))
    vts(T.PJ[:, 3:4], T.PI4[:, 3:4], 4, None, OP.arith_shift_right, R=("PI4",), W=("PJ3",))
    vcp(T.M16[:], T.M16i[:], ("M16i",), ("M16",))
    vcp(T.PC[:], T.PJ[:], ("PJ0", "PJ1", "PJ2", "PJ3"), ("PC",))
    vts(T.h16[:, 0:4], T.IH[:, 0:4], 0.0, None, OP.is_ge, R=("IH",), W=("on4",))
    vts(T.LEs[:, 0:1], T.IH[:, 0:1], 0.0, None, OP.mult, R=("IH",), W=("LEs0",))
    vts(T.mh[:, 0:1], T.PC[0:16, 0:1], 8.0, None, OP.is_lt, R=("PC",), W=("mh0",))
    vts(T.mh[:, 1:2], T.PC[0:16, 0:1], 8.0, None, OP.is_ge, R=("PC",), W=("mh1",))
    vts(T.R8[:], T.IH[0:16, 0:8], T.PC[0:16, 1:2], None, OP.is_equal, R=("IH", "PC"), W=("R8",))
    vts(T.SL[:], T.IH[:], T.PC[:, 0:1], None, OP.is_gt, R=("IH", "PC"), W=("SL",))
    vts(T.SU[:], T.IH[:], T.PC[:, 0:1], None, OP.is_lt, R=("IH", "PC"), W=("SU",))

    for h in range(2):
        vts(T.kl[:, h::2], T.kS[:], T.mh[:, h:h + 1], None, OP.mult, R=("kS", "mh%d" % h), W=("kl%d" % h,))
    mm(T.psA[:, 0:8], T.kl[:], T.R8[:], ("kl0", "kl1", "R8"), ("psA",))
    O8 = ["O%d" % t for t in range(8)]
    for t in range(8):
        vts(T.O[:, t::8], T.IH[:, 0:64], T.psA[:, t:t + 1], None, OP.is_equal, R=("IH", "psA"), W=(O8[t],))
    op("v", v.tensor_tensor_scan, O8, ("S",), T.S[:], T.O[:], T.O[:], 0.0, OP.add, OP.max)
    vcp(T.LE2[:, 0:64], T.S[:, 7::8], ("S",), ("LE2a",))
    vcp(T.LE2[:, 64:128], T.S[:, 7::8], ("S",), ("LE2b",))
    vcp(T.LEs[:, 1:64], T.S[:, 7:504:8], ("S",), ("LEs1",))
    mm(T.psH[:, 0:4], T.LE2[:], T.h16[:, 0:4], ("LE2a", "LE2b", "on4"), ("psH",))
    mm(T.psB[:, 0:64], T.SL[:], T.LE2[:, 0:64], ("SL", "LE2a"), ("psB",), True, False)
    mm(T.psB[:, 0:64], T.SU[:], T.LEs[:], ("SU", "LEs0", "LEs1"), ("psB",), False, True)
    vcp(T.Cc[:, 4 * rank:4 * rank + 4], T.psH[:, 0:4], ("psH",), ("Cown",))

    n = 0
    for i in range(6):
        if i == 3:
            reads("p", ("Cown",))
            n += send([idx], off, "Cc", 4 * rank, 4, "harr")
            n += send(direct, off, "Cc", 4 * rank, 4, "harr")
        need("p", [("x%d" % (i // 2), 16)])
        n += send([relays[i]], inner if i < 3 else off, "XW", TC * rank + BEG[i], WID[i], "xarr")

    for t in range(8):
        vtt(T.SB[:, 64 * t:64 * t + 64], T.S[:, t::8], T.psB[:, 0:64], OP.add, R=("S", "psB"), W=("SB%d" % t,))
    for t in (4, 5, 6, 7, 0, 1, 2, 3):
        vtt(T.Wk[:, 64 * t:64 * t + 64], T.SB[:, 64 * t:64 * t + 64], T.O[:, t::8], OP.mult, R=("SB%d" % t, O8[t]), W=("Wk%d" % t,))
    for t in range(4):
        op("v", v.tensor_reduce, ("Wk%d" % t,), ("pos%d" % t,), T.pos[:, t:t + 1], T.Wk[:, 64 * t:64 * t + 64], AxisListType.X, OP.add)
    for t in range(4, 8):
        op("a", g.scalar.activation, ("Wk%d" % t,), ("pos%d" % t,), T.yS[:, 64 * t:64 * t + 64], T.Wk[:, 64 * t:64 * t + 64],
           ACT.Copy, accum_out=T.pos[:, t:t + 1])
    vts(T.pi[:], T.pos[:], 1.0, None, OP.subtract, R=["pos%d" % t for t in range(8)], W=("pi",))
    vts(T.hl[:, 0:8], T.pi[:], 4, None, OP.arith_shift_right, R=("pi",), W=("hl0",))
    vts(T.hl[:, 8:16], T.pi[:], 15, None, OP.bitwise_and, R=("pi",), W=("hl1",))
    vcp(T.hlF[:], T.hl[:], ("hl0", "hl1"), ("hlF",))
    for t in range(8):
        vts(T.Ah[:, 128 * t:128 * t + 128], T.M16[:], T.hlF[:, 8 + t:9 + t], None, OP.is_equal, R=("M16", "hlF"), W=("A%d" % t,))
        vts(T.Bh[:, 64 * t:64 * t + 64], T.IH[:, 0:64], T.hlF[:, t:t + 1], T.JI[:, t:t + 1], OP.is_equal, OP.mult,
            R=("IH", "hlF", "JI"), W=("B%d" % t,))
        mm(T.psL[:, 0:64], T.Ah[:, 128 * t:128 * t + 128], T.Bh[:, 64 * t:64 * t + 64], ("A%d" % t, "B%d" % t), ("psL",), t == 0, t == 7)
    vcp(T.Lw[:, 64 * rank:64 * rank + 64], T.psL[:, 0:64], ("psL",), ("Lown",))
    reads("p", ("Lown",))
    n += send([idx], off, "Lw", 64 * rank, 64, "larr")
    n += send(direct, off, "Lw", 64 * rank, 64, "larr")

    vts(T.shf[:], T.IH[:], T.PC[:, 0:1], 1.0, OP.subtract, OP.is_equal, R=("IH", "PC"), W=("shf",))
    op("v", v.memset, (), ("shf",), T.shf[:, 64:65], 0.0)
    for b in range(8):
        vts(T.i1k[:, 128 * b:128 * b + 128], T.IH[:], float(128 * b), None, OP.add, R=("IH",), W=("i1k%d" % b,))
    op("v", v.memset, (), ("on16",), T.on16[:], 1.0)
    vts(T.rv[:], T.i1k[:, 0:96], 0.0, 1024.0, OP.mult, OP.add, R=("i1k0",), W=("rv0", "rv1", "rv2"))
    vts(sm[:, DR:DR + 1], T.PC[:, 0:1], 64.0, 6144.0, OP.is_ge, OP.mult, R=("PC",), W=("dr0",))
    vts(sm[:, DR + 1:DR + 2], T.PC[:, 0:1], 0.0, 5120.0, OP.is_equal, OP.mult, R=("PC",), W=("dr1",))
    vts(sm[:, DR:DR + 1], sm[:, DR:DR + 1], sm[:, DR + 1:DR + 2], -5120.0, OP.add, OP.add, R=("dr0", "dr1"), W=("dr0",))
    vts(T.rv[:, 1:32:2], T.on16[:], sm[:, DR:DR + 1], None, OP.mult, R=("on16", "dr0"), W=("rv0",))
    op("v", v.memset, (), ("PX0",), sm[:, PX:PX + 1], 0.0)
    vts(T.gI[:], T.II[:], 4, None, OP.arith_shift_right, R=("II",), W=("gI",))
    vts(sm[:, PQ:PQ + 1], T.PC[:, 0:1], float(TC * rank), None, OP.add, R=("PC",), W=("pq",))
    vts(T.Qc[:], T.gI[:], 128.0, sm[:, PQ:PQ + 1], OP.mult, OP.add, R=("gI", "pq"), W=("Qc",))
    vts(T.e16[:], T.M16[:], T.PC[:, 2:3], None, OP.is_equal, R=("M16", "PC"), W=("e16",))
    vts(T.m8[:], T.IH[:, 0:8], T.PC[:, 3:4], None, OP.is_equal, R=("IH", "PC"), W=("m8",))
    vcp(T.h16[:, 8:16], T.m8[:], ("m8",), ("m8h",))
    vts(T.id16[:], T.IH[:], T.PC[:, 0:1], None, OP.is_equal, R=("IH", "PC"), W=("id16",))
    vts(T.rst[:], T.M16[:], 0.0, None, OP.not_equal, R=("M16",), W=("rst",))

    narr = 5 * _engines(off)
    wr["Call"] = [("harr", narr)] + wr["Cown"]
    op("v", v.tensor_tensor_scan, ("Call",), ("PX1",), sm[:, PX + 1:PX + 7], T.Cc[:, 0::4], T.Cc[:, 0::4], 0.0, OP.add, OP.max)
    mm(T.psA[:, 0:7], T.shf[:], sm[:, PX:PX + 7], ("shf", "PX0", "PX1"), ("psA",))
    vcp(sm[:, SH:SH + 7], T.psA[:, 0:7], ("psA",), ("ShS",))
    vtt(sm[0:64, TG:TG + 3], sm[0:64, PX:PX + 6:2], sm[0:64, SH:SH + 6:2], OP.subtract, R=("PX0", "PX1", "ShS"), W=("tg0",))
    vtt(sm[64:128, TG:TG + 3], sm[64:128, PX + 1:PX + 6:2], sm[64:128, SH + 1:SH + 6:2], OP.subtract, R=("PX1", "ShS"), W=("tg1",))
    vtt(sm[:, CS:CS + 6], sm[:, SH + 1:SH + 7], sm[:, SH:SH + 6], OP.subtract, R=("ShS",), W=("CS",))
    vts(sm[:, TH:TH + 3], sm[:, TG:TG + 3], sm[:, SH + 6:SH + 7], float(-TC * rank), OP.add, OP.add, R=("tg0", "tg1", "ShS"), W=("Th",))
    vtt(sm[64:128, DV:DV + 3], sm[64:128, CS + 1:CS + 6:2], T.Cc[64:128, 0:17:8], OP.subtract, R=("CS", "Call"), W=("dv0",))
    vtt(sm[0:64, DV + 1:DV + 3], sm[0:64, CS + 2:CS + 5:2], T.Cc[0:64, 4:13:8], OP.subtract, R=("CS", "Call"), W=("dv1",))
    vtt(sm[0:64, DV:DV + 1], sm[0:64, CS:CS + 1], sm[0:64, CS + 5:CS + 6], OP.subtract, R=("CS",), W=("dv2",))
    for s in range(3):
        vts(T.rv[:, 32 * s:32 * s + 32:2], T.on16[:], sm[:, DV + s:DV + s + 1], None, OP.mult,
            R=("on16", "dv0", "dv1", "dv2"), W=("rv%d" % s,))
    for part in range(4):
        for s in range(3):
            a = 256 * part
            vts(T.U[:, 1024 * s + a:1024 * s + a + 256], T.i1k[:, a:a + 256], sm[:, TH + s:TH + s + 1], None, OP.is_ge,
                R=("i1k%d" % (2 * part), "i1k%d" % (2 * part + 1), "Th"), W=("U%d%d" % (s, part),))
    for gr in range(8):
        for s in range(3):
            a = 1024 * s + 128 * gr
            mm(T.psV[:, 32 * gr:32 * gr + 32], T.U[:, a:a + 128], T.rv[:, 32 * s:32 * s + 32],
               ("U%d%d" % (s, gr // 2), "rv%d" % s), ("psV%d" % gr,), s == 0, s == 2)
    PV = ["psV%d" % gr for gr in range(8)]
    vtt(T.f1[:], T.psV[:, 0:256:2], T.Qc[:], OP.add, R=PV + ["Qc"], W=("f1",))
    vtt(T.fi[:], T.psV[:, 1:256:2], T.f1[:], OP.add, R=PV + ["f1"], W=("fi",))
    vts(T.hi[:], T.fi[:], 4, None, OP.arith_shift_right, R=("fi",), W=("hi",))
    vts(T.lo[:], T.fi[:], 15, None, OP.bitwise_and, R=("fi",), W=("lo",))
    vtt(T.hm[:], T.hi[:], T.e16[:], OP.mult, R=("hi", "e16"), W=("hm",))
    mm(T.psO[:, 0:8], T.hm[:], T.h16[:, 8:16], ("hm", "m8h"), ("psO",))
    vtt(T.lm[:], T.lo[:], T.M16i[:], OP.is_equal, R=("lo", "M16i"), W=("lm",))
    vcp(T.off1[:], T.psO[:, 0:8], ("psO",), ("off1",))
    wr["Lall"] = [("larr", narr)] + wr["Lown"]
    vcp(T.G[:], T.Lw[:, 0:64 * NR].indirect(T.off1[:, 0:8]), ("Lall", "off1"), ("G",))
    mm(T.psG[:, 0:128], T.G[:], T.id16[:], ("G", "id16"), ("psG",))
    for b in range(8):
        vts(T.lr[:, 64 + b::8], T.psV[:, 1:256:32], T.m8[:, b:b + 1], None, OP.mult, R=PV + ["m8"], W=("lrR%d" % b,))
    vtt(T.GM[:], T.psG[:, 0:128], T.lm[:], OP.mult, R=("psG", "lm"), W=("GM",))
    op("v", v.tensor_tensor_scan, ("GM", "rst"), ("GS",), T.GS[:], T.rst[:], T.GM[:], 0.0, OP.mult, OP.add)
    mm(T.psF[:, 0:64], T.e16[:], T.lr[:, 64:128], ["e16"] + ["lrR%d" % b for b in range(8)], ("psF",), True, False)
    for b in range(8):
        vts(T.lr[:, b:64:8], T.GS[:, 15::16], T.m8[:, b:b + 1], None, OP.mult, R=("GS", "m8"), W=("lr%d" % b,))
    mm(T.psF[:, 0:64], T.e16[:], T.lr[:, 0:64], ["e16"] + ["lr%d" % b for b in range(8)], ("psF",), False, True)
    vcp(T.lst[:], T.psF[:, 0:64], ("psF",), ("lst",))

    wr["XW"] = [("xarr", 5 * 6 * _engines(off))] + [("x%d" % i, 16) for i in range(3)]
    for i in range(2):
        vcp(T.yS[:, 256 * i:256 * i + 256], T.XW[:].indirect(T.lst[:, 16 * i:16 * i + 16]), ("XW", "lst"), ("y%d" % i,))
    for i in range(2, 4):
        op("a", g.scalar.activation, ("XW", "lst"), ("y%d" % i,), T.yS[:, 256 * i:256 * i + 256],
           T.XW[:].indirect(T.lst[:, 16 * i:16 * i + 16]), ACT.Copy)
    for i in range(2):
        reads("y", ("y%d" % i,))
        g.sync.dma_start(T.y[:, 256 * i:256 * i + 256], T.yS[:, 256 * i:256 * i + 256]).then_inc(T.sem.ysy, 16)
    for i in range(2, 4):
        reads("a", ("y%d" % i,))
        g.scalar.dma_start(T.y[:, 256 * i:256 * i + 256], T.yS[:, 256 * i:256 * i + 256]).then_inc(T.sem.ysc, 16)
    g.sync.wait_ge(T.sem.ysy, 32)
    g.scalar.wait_ge(T.sem.ysc, 32)
    g.wait_ge(T.sem.loc, n)
    for s, c in cnt.items():
        if seen.get(("p", s), 0) < c:
            g.wait_ge(T.sem[s], c)
